import numpy as np
import ml_dtypes


def mxq(x, axis, fmt="e4m3"):
    dtype, down = {"e4m3": (ml_dtypes.float8_e4m3fn, 7), "e5m2": (ml_dtypes.float8_e5m2, 14)}[fmt]
    v = np.moveaxis(np.asarray(x, np.float32).astype(ml_dtypes.bfloat16).astype(np.float64), axis, -1)
    blocks = v.reshape(v.shape[:-1] + (-1, 32))
    amax = np.abs(blocks).max(-1, keepdims=True)
    byte = np.maximum(np.where(amax > 0, np.frexp(amax)[1] - 1 + 127, 0) - down, 1)
    scale = np.exp2(byte - 127.0)
    codes = (blocks / scale).astype(np.float32).astype(dtype).astype(np.float64)
    return np.moveaxis((codes * scale).reshape(v.shape), -1, axis)


WIDE = False


def mx_kscale(k):
    if not WIDE:
        return np.ones(k)
    levels = np.array([10, -10, 5, -5, 0])
    if k % 512:
        return np.exp2(np.random.permutation(np.resize(levels, k // 32))).repeat(32)
    a = np.empty((k // 512, 16))
    for p in range(k // 512):
        a[p, :8] = np.random.permutation(np.resize(levels, 8))
        for g in range(8):
            far = levels[np.abs(levels - a[p, g]) >= 10]
            a[p, g + 8] = far[np.random.randint(len(far))]
    return np.exp2(a.ravel()).repeat(32)


def f64(x):
    return np.asarray(x).astype(np.float64)


def striped(idx):
    return np.tile(idx.reshape(-1, 16).T, (8, 1)).astype(np.uint16)


def unstriped(offs):
    return offs[:16].T.reshape(-1).astype(np.int64)


def striped8(idx):
    return np.concatenate([x.reshape(-1, 16).T for x in idx]).astype(np.uint16)


def runs(offs, k):
    lists = np.stack([offs[16 * r : 16 * r + 16].T.reshape(-1) for r in range(8)]).astype(np.int64)
    return lists[np.arange(k) % 512 // 64]


def pack_weight(w):
    k, n = w.shape
    w = f64(np.asarray(w, np.float32).astype(ml_dtypes.bfloat16)).reshape(k // 32, 32, n)
    amax = np.abs(w).max(1)
    byte = np.clip(np.where(amax > 0, np.frexp(amax)[1] - 1 + 127 - 7, 1), 1, 254)
    scaled = (w * np.exp2(127.0 - byte)[:, None, :]).reshape(k, n).astype(np.float32)
    words = np.ascontiguousarray(scaled.reshape(k // 512, 128, 4, n).transpose(0, 1, 3, 2)).astype(ml_dtypes.float8_e4m3fn).view(np.uint8)
    return words, np.ascontiguousarray(byte.astype(np.uint8).reshape(k // 512, 16, n))


def unpack_weight(words, scales):
    g, p, n, _ = words.shape
    vals = np.ascontiguousarray(words).view(ml_dtypes.float8_e4m3fn).astype(np.float64) * np.repeat(np.exp2(scales.astype(np.float64) - 127.0), 8, axis=1)[..., None]
    return vals.transpose(0, 1, 3, 2).reshape(g * 512, n)


K, T, S, N, H, G, W, U = 512, 1024, 256, 512, 512, 2048, 1024, 192


def setup_inputs():
    n = np.random.standard_normal
    s = mx_kscale(K)[:, None]
    u = mx_kscale(K)
    packed_xT = pack_weight(n((K, T)) * s)
    packed_dT = pack_weight(n((K, G)) / s)
    return {
        "x_words": packed_xT[0],
        "x_scales": packed_xT[1],
        "w1": (n((K, H)) / np.sqrt(K) / s).astype(np.float32),
        "d_words": packed_dT[0],
        "d_scales": packed_dT[1],
        "tau": np.random.uniform(0.3, 0.9, (H, 1)).astype(np.float32),
        "tau2": np.random.uniform(0.3, 0.9, (H, 1)).astype(np.float32),
        "gn": (np.random.uniform(0.5, 1.5, (H, 1)) * u[:, None]).astype(np.float32),
        "gk": (np.random.uniform(0.5, 1.5, (H, 1)) * u[:, None]).astype(np.float32),
        "w2": (n((H, N)) / np.sqrt(2 * H) / u[:, None]).astype(np.float32),
        "w3": (n((H, N)) / np.sqrt(2 * H) / u[:, None]).astype(np.float32),
        "offs": striped(np.random.permutation(T)[:S]),
        "kidx": striped8(np.random.randint(0, G, (8, H))),
        "two": striped(np.random.permutation(T)[:S]),
        "n1": striped(np.random.randint(0, S, W)),
        "n2": striped(np.random.permutation(S)),
        "n3": striped(np.random.permutation(S)),
        "n4": striped(np.random.permutation(S)[:U]),
        "n5": striped(np.random.permutation(S)[:U]),
    }


def reference(x_words, x_scales, w1, d_words, d_scales, tau, tau2, gn, gk, w2, w3, offs, kidx, two, n1, n2, n3, n4, n5):
    xq = unpack_weight(x_words, x_scales)[:, unstriped(offs)]
    y = mxq(f64(w1), 0, "e4m3").T @ xq
    top = y.max(axis=1, keepdims=True)
    ea = np.exp(f64(tau) * (y[:, unstriped(n1)] - top))
    ms = ea.reshape(H, S, 4).sum(axis=2)
    z = f64(gn) * (np.log(ms + 0.25) - (0.5 * y))
    d_kidx = unpack_weight(d_words, d_scales)[np.arange(K)[:, None], runs(kidx, K)]
    x_two = unpack_weight(x_words, x_scales)[:, unstriped(two)]
    s = 0.0625 * (d_kidx.T @ x_two)
    top2 = s.max(axis=1, keepdims=True)
    ea2 = np.exp(f64(tau2) * (s[:, unstriped(n2)] - top2))
    sm = s * ea2
    ds = np.zeros((H, S))
    ds[:, unstriped(n3)] = sm
    z2 = f64(gk) * (2.0 * ds - (0.5 * s))
    h = mxq(f64(w2), 0, "e4m3").T @ mxq(z, 0, "e4m3") + mxq(f64(w3), 0, "e4m3").T @ mxq(z2, 0, "e4m3")
    old = h[:, unstriped(n4)]
    pa = h[:, unstriped(n5)]
    ra = old - (0.5 * pa)
    out = h.copy()
    out[:, unstriped(n4)] = ra
    return out

@@ -1,0 +1,295 @@
+from contextlib import ExitStack
+
+import concourse.mybir as mybir
+from concourse.masks import make_identity
+
+K, T, S, N, H, G, W, U = 512, 1024, 256, 512, 512, 2048, 1024, 192
+FLOPS = 2 * (K * H * S + K * H * S + H * N * S + H * N * S)
+
+F32 = mybir.dt.float32
+BF16 = mybir.dt.bfloat16
+I32 = mybir.dt.int32
+U32 = mybir.dt.uint32
+U16 = mybir.dt.uint16
+U8 = mybir.dt.uint8
+FP8X4 = mybir.dt.float8_e4m3fn_x4
+MULT = mybir.AluOpType.mult
+ADD = mybir.AluOpType.add
+MAX = mybir.AluOpType.max
+COPY = mybir.ActivationFunctionType.Copy
+EXP = mybir.ActivationFunctionType.Exp
+LN = mybir.ActivationFunctionType.Ln
+
+P = 128
+R = 4
+YW = 1024
+SW = 512
+
+
+def tile_picked_jkeyeglesdkdif_none_p_kernel(
+    tc, x_words, x_scales, w1, d_words, d_scales, tau, tau2, gn, gk, w2, w3, offs, kidx, two, n1, n2, n3, n4, n5, out
+):
+    nc = tc.nc
+    with ExitStack() as ctx:
+        lists = ctx.enter_context(tc.tile_pool(name="lists", bufs=1))
+        sb = ctx.enter_context(tc.tile_pool(name="sb", bufs=1))
+        ps = ctx.enter_context(tc.psum_pool(name="ps", bufs=1))
+
+        def tile(name, shape, dtype, tag=None):
+            return sb.tile(shape, dtype, name=name, tag=tag or name, align_bytes=64)
+
+        def bank(name, tag):
+            return ps.tile([P, 512], F32, name=name, tag=tag)
+
+        def load_list(name, src):
+            t = lists.tile(list(src.shape), U16, name=name, tag=name)
+            nc.sync.dma_start(t[:], src)
+            return t
+
+        def load_col(name, src):
+            t = tile(name, [P, R], F32)
+            nc.sync.dma_start(t[:], src.rearrange("(p t) o -> p (t o)", t=R))
+            return t
+
+        xs_win = tile("xs_win", [P, T], U8)
+        nc.gpsimd.memset(xs_win[:].bitcast(I32), 0)
+        ds_win = tile("ds_win", [P, G], U8)
+        nc.vector.memset(ds_win[:].bitcast(I32), 0)
+        y_win = [tile(f"y_win{t}", [P, YW], F32) for t in range(R)]
+        for t in range(R):
+            nc.vector.memset(y_win[t][:, 3 * S :], 0.0)
+        w1_raw = [y_win[t][:, S : 3 * S].rearrange("p (j c) -> p j c", j=R) for t in range(R)]
+
+        def load_w1(t):
+            nc.sync.dma_start(w1_raw[t], w1.rearrange("(p j) c -> p j c", j=R)[:, :, P * t : P * (t + 1)])
+
+        offs_t = load_list("offs_t", offs)
+        xs_rows = x_scales[0].bitcast(I32)
+        for q in range(4):
+            nc.scalar.dma_start(xs_win[32 * q : 32 * q + 4, :].bitcast(I32), xs_rows[4 * q : 4 * q + 4, :])
+        load_w1(0)
+        xw_win = tile("xw_win", [P, T], U32)
+        nc.sync.dma_start(xw_win[:].bitcast(I32), x_words[0].rearrange("p n r -> p (n r)").bitcast(I32))
+        tau_c = tile("tau_c", [P, R], F32)
+        with nc.allow_non_contiguous_dma(reason="one value a row, rows in plain order"):
+            nc.sync.dma_start(tau_c[:], tau.rearrange("(t p) o -> p (t o)", p=P))
+        load_w1(1)
+        n1_t = load_list("n1_t", n1)
+        load_w1(2)
+        load_w1(3)
+        ds_rows = d_scales[0].bitcast(I32)
+        for e in range(2):
+            nc.sync.dma_start(ds_win[e:P:16, :].bitcast(I32), ds_rows[e:16:2, :])
+        kidx_t = load_list("kidx_t", kidx)
+        two_t = load_list("two_t", two)
+        dw_win = tile("dw_win", [P, G], U32)
+        nc.sync.dma_start(dw_win[:].bitcast(I32), d_words[0].rearrange("p n r -> p (n r)").bitcast(I32))
+        tau2_c = load_col("tau2_c", tau2)
+        n2_t = load_list("n2_t", n2)
+        gk_c = load_col("gk_c", gk)
+        gn_c = load_col("gn_c", gn)
+        w2_raw = tile("w2_raw", [P, R, N], F32)
+        nc.sync.dma_start(w2_raw[:], w2.rearrange("(p j) c -> p j c", j=R))
+        n3_t = load_list("n3_t", n3)
+        n4_t = load_list("n4_t", n4)
+        n5_t = load_list("n5_t", n5)
+
+        ident = tile("ident", [P, P], F32)
+        make_identity(nc, ident[:])
+        s_win = [tile(f"s_win{t}", [P, SW], F32) for t in range(R)]
+        for t in range(R):
+            nc.gpsimd.memset(s_win[t][:, S:], 0.0)
+
+        xs1 = tile("xs1", [P, S], U8)
+        nc.vector.tensor_copy(xs1[:], xs_win[:].indirect(offs_t[:]))
+
+        def interleave(raw, name, tag=None):
+            bf = tile(name, [P, raw.shape[2], R], BF16, tag=tag)
+            return bf, bf[:].rearrange("p (c i) j -> p c j i", i=4), raw.rearrange("p j (c i) -> p c j i", i=4)
+
+        def quantise(name, bf):
+            width = bf.shape[1]
+            codes = tile(name + "_c", [P, width], U32)
+            scales = tile(name + "_s", [P, width], U8)
+            nc.vector.quantize_mx(out=codes[:].bitcast(FP8X4), scales=scales[:], in_=bf.rearrange("p c j -> p (c j)"))
+            return codes, scales
+
+        top1 = [tile(f"top1_{t}", [P, 1], F32) for t in range(R)]
+        nb1 = tile("nb1", [P, R], F32)
+        xw1 = tile("xw1", [P, S], U32)
+
+        def project(t, w1_c, w1_s):
+            y_ps = bank(f"y_ps{t}", f"A{t}")
+            nc.tensor.matmul_mx(
+                out=y_ps[:, :S], lhsT=w1_c.bitcast(FP8X4), lhsT_scale=w1_s,
+                rhs=xw1[:].bitcast(FP8X4), rhs_scale=xs1[:], start=True, stop=True,
+            )
+            nc.vector.tensor_scalar(
+                y_win[t][:, :S], y_ps[:, :S], 1.0, None, MULT, MAX, accum_out=top1[t][:]
+            )
+            nc.vector.tensor_scalar(nb1[:, t : t + 1], top1[t][:], tau_c[:, t : t + 1], -1.0, MULT, MULT)
+
+        for t in range(2):
+            bf, dst, src = interleave(w1_raw[t], f"w1_bf{t}")
+            nc.scalar.activation(dst, src, COPY)
+            codes, scales = quantise(f"w1_{t}", bf[:])
+            if t == 0:
+                nc.vector.tensor_copy(xw1[:], xw_win[:].indirect(offs_t[:]))
+            project(t, codes[:], scales[:])
+
+        w1_q = []
+        for t in range(2, R):
+            bf, dst, src = interleave(w1_raw[t], f"w1_bf{t}")
+            nc.vector.tensor_copy(dst, src)
+            w1_q.append(bf)
+        for t in range(2, R):
+            codes, scales = quantise(f"w1_{t}", w1_q[t - 2][:])
+            project(t, codes[:], scales[:])
+
+        ds_g = tile("ds_g", [P, H], U8, tag="top1_3")
+        nc.vector.tensor_copy(ds_g[:], ds_win[:].indirect(kidx_t[:]))
+        ds_d = tile("ds_d", [P, H], U8)
+        nc.vector.tensor_copy(
+            ds_d[:].rearrange("p (t m) -> p m t", t=R), ds_g[:].rearrange("p (m t) -> p m t", t=R)
+        )
+        ds_p = tile("ds_p", [P, H], U8)
+        nc.vector.tensor_copy(ds_p[:].bitcast(I32), ds_d[:].bitcast(I32))
+        for e in range(2):
+            nc.sync.dma_start(ds_p[2 + e : P : 32, :].bitcast(I32), ds_d[16 + e : P : 32, :].bitcast(I32))
+
+        w3_raw = tile("w3_raw", [P, R, N], F32, tag="ds_d")
+        nc.sync.dma_start(w3_raw[:], w3.rearrange("(p j) c -> p j c", j=R))
+        xw2 = tile("xw2", [P, S], U32, tag="top1_2")
+        nc.vector.tensor_copy(xw2[:], xw_win[:].indirect(two_t[:]))
+        xs2 = tile("xs2", [P, S], U8, tag="top1_1")
+        nc.vector.tensor_copy(xs2[:], xs_win[:].indirect(two_t[:]))
+        dw_g = tile("dw_g", [P, H], U32, tag="top1_3")
+        nc.vector.tensor_copy(dw_g[:], dw_win[:].indirect(kidx_t[:]))
+        dw_d = tile("dw_d", [P, H], U32)
+        nc.vector.tensor_copy(
+            dw_d[:].rearrange("p (t m) -> p m t", t=R), dw_g[:].rearrange("p (m t) -> p m t", t=R)
+        )
+        top2 = [tile(f"top2_{t}", [P, 1], F32) for t in range(R)]
+        nb2 = tile("nb2", [P, R], F32, tag="hold")
+        for t in range(R):
+            s_ps = bank(f"s_ps{t}", ["A0", "A1", "A2", "B3"][t])
+            cols = slice(P * t, P * (t + 1))
+            nc.tensor.matmul_mx(
+                out=s_ps[:, :S], lhsT=dw_d[:, cols].bitcast(FP8X4), lhsT_scale=ds_p[:, cols],
+                rhs=xw2[:].bitcast(FP8X4), rhs_scale=xs2[:], start=True, stop=True,
+            )
+            nc.vector.tensor_scalar(
+                s_win[t][:, :S], s_ps[:, :S], 0.0625, None, MULT, MAX, accum_out=top2[t][:]
+            )
+            nc.vector.tensor_scalar(nb2[:, t : t + 1], top2[t][:], tau2_c[:, t : t + 1], -1.0, MULT, MULT)
+
+        ms_ps = [bank("ms_ps0", "A3"), bank("ms_ps1", "B3")]
+        for t in range(R):
+            for h in range(2):
+                ea = tile(f"ea{t}{h}", [P, W // 2], F32)
+                nc.scalar.activation(
+                    ea[:], y_win[t][:].indirect(n1_t[:, 32 * h : 32 * (h + 1)]), EXP,
+                    bias=nb1[:, t : t + 1], scale=tau_c[:, t : t + 1],
+                )
+                blk = 2 * h + t % 2
+                for e in range(4):
+                    nc.tensor.matmul(
+                        ms_ps[t // 2][:, P * blk : P * (blk + 1)], lhsT=ea[:, e :: 4], rhs=ident[:],
+                        start=(e == 0), stop=(e == 3), is_transpose=True,
+                    )
+
+        yt_ps = [bank("yt_ps0", "B1"), bank("yt_ps1", "B2")]
+        for t in range(R):
+            for h in range(2):
+                blk = 2 * h + t % 2
+                nc.tensor.transpose(yt_ps[t // 2][:, P * blk : P * (blk + 1)], y_win[t][:, P * h : P * (h + 1)], ident[:])
+
+        gk2 = tile("gk2", [P, R], F32)
+        nc.vector.tensor_scalar(gk2[:], gk_c[:], 2.0, None, MULT)
+        gkh = tile("gkh", [P, R], F32)
+        nc.vector.tensor_scalar(gkh[:], gk_c[:], -0.5, None, MULT)
+        sm = []
+        for t in range(R):
+            ea2 = tile(f"ea2{t}", [P, S], F32)
+            nc.scalar.activation(
+                ea2[:], s_win[t][:].indirect(n2_t[:]), EXP, bias=nb2[:, t : t + 1], scale=tau2_c[:, t : t + 1]
+            )
+            sm.append(tile(f"sm{t}", [P, S], F32))
+            nc.vector.scalar_tensor_tensor(sm[t][:], s_win[t][:, :S], gk2[:, t : t + 1], ea2[:], MULT, MULT)
+
+        bf, dst, src = interleave(w2_raw[:], "w2_bf", "top2_2")
+        nc.vector.tensor_copy(dst, src)
+        bf3, dst, src = interleave(w3_raw[:], "w3_bf", "top2_3")
+        nc.vector.tensor_copy(dst, src)
+        w2_c, w2_s = quantise("w2", bf[:])
+        w3_c, w3_s = quantise("w3", bf3[:])
+
+        ln_t = tile("ln_t", [P, 2, 512], F32, tag="hold")
+        u_t = tile("u_t", [P, 2, H], F32)
+        for u in range(2):
+            nc.scalar.activation(ln_t[:, u, :], ms_ps[u][:], LN, bias=0.25)
+            nc.vector.scalar_tensor_tensor(
+                u_t[:, :, 256 * u : 256 * (u + 1)], yt_ps[u][:].rearrange("p (h c) -> p h c", h=2), -0.5,
+                ln_t[:, u, :].rearrange("p (h c) -> p h c", h=2), MULT, ADD,
+            )
+        z_bf = tile("z_bf", [P, S, R], BF16, tag="top2_3")
+        for h in range(2):
+            u_ps = bank(f"u_ps{h}", f"A{h}")
+            for t in range(R):
+                nc.tensor.transpose(u_ps[:, P * t : P * (t + 1)], u_t[:, h, t::R], ident[:])
+            nc.vector.tensor_tensor(
+                z_bf[:, P * h : P * (h + 1), :], u_ps[:].rearrange("p (t j) -> p j t", t=R),
+                gn_c[:].unsqueeze(1).to_broadcast([P, P, R]), MULT,
+            )
+        z_c, z_s = quantise("z", z_bf[:])
+
+        z2f = tile("z2f", [P, R - 1, S], F32, tag="top2_3")
+        z2_bf = tile("z2_bf", [P, S, R], BF16)
+        for t in range(R):
+            ds = tile(f"ds{t}", [P, SW], F32)
+            nc.scalar.activation(ds[:].indirect(n3_t[:]), sm[t][:], COPY)
+            dst = z2f[:, t, :] if t < R - 1 else z2_bf[:, :, t]
+            nc.vector.scalar_tensor_tensor(dst, s_win[t][:, :S], gkh[:, t : t + 1], ds[:, :S], MULT, ADD)
+            if t == R - 2:
+                nc.vector.tensor_copy(
+                    z2_bf[:, :, : R - 1].rearrange("p (c i) t -> p c t i", i=4),
+                    z2f[:].rearrange("p t (c i) -> p c t i", i=4),
+                )
+        z2_c, z2_s = quantise("z2", z2_bf[:])
+
+        h_ps = [bank(f"h_ps{m}", tag) for m, tag in enumerate(["A2", "B0", "A3", "B1"])]
+        for m in range(R):
+            cols = slice(P * m, P * (m + 1))
+            nc.tensor.matmul_mx(
+                out=h_ps[m][:, :S], lhsT=w2_c[:, cols].bitcast(FP8X4), lhsT_scale=w2_s[:, cols],
+                rhs=z_c[:].bitcast(FP8X4), rhs_scale=z_s[:], start=True, stop=False,
+            )
+        h_win = []
+        for m in range(R):
+            cols = slice(P * m, P * (m + 1))
+            nc.tensor.matmul_mx(
+                out=h_ps[m][:, :S], lhsT=w3_c[:, cols].bitcast(FP8X4), lhsT_scale=w3_s[:, cols],
+                rhs=z2_c[:].bitcast(FP8X4), rhs_scale=z2_s[:], start=False, stop=True,
+            )
+            h_win.append(tile(f"h_win{m}", [P, S], F32))
+            nc.vector.tensor_copy(h_win[m][:], h_ps[m][:, :S])
+
+        ra = []
+
+        def fetch(m):
+            old = tile(f"old{m}", [P, U], F32)
+            nc.scalar.activation(old[:], h_win[m][:].indirect(n4_t[:]), COPY)
+            pa = tile(f"pa{m}", [P, U], F32)
+            nc.scalar.activation(pa[:], h_win[m][:].indirect(n5_t[:]), COPY)
+            ra.append(tile(f"ra{m}", [P, U], F32))
+            nc.vector.scalar_tensor_tensor(ra[m][:], pa[:], -0.5, old[:], MULT, ADD)
+
+        def put(m):
+            nc.scalar.activation(h_win[m][:].indirect(n4_t[:]), ra[m][:], COPY)
+            nc.sync.dma_start(out[P * m : P * (m + 1), :], h_win[m][:])
+
+        fetch(0)
+        for m in range(1, R):
+            fetch(m)
+            put(m - 1)
+        put(R - 1)

@@ -66,7 +66,7 @@ def tile_picked_jkeyeglesdkdif_none_p_kernel(
         offs_t = load_list("offs_t", offs)
         xs_rows = x_scales[0].bitcast(I32)
         for q in range(4):
-            nc.scalar.dma_start(xs_win[32 * q : 32 * q + 4, :].bitcast(I32), xs_rows[4 * q : 4 * q + 4, :])
+            (nc.sync if q == 0 else nc.scalar).dma_start(xs_win[32 * q : 32 * q + 4, :].bitcast(I32), xs_rows[4 * q : 4 * q + 4, :])
         load_w1(0)
         xw_win = tile("xw_win", [P, T], U32)
         nc.sync.dma_start(xw_win[:].bitcast(I32), x_words[0].rearrange("p n r -> p (n r)").bitcast(I32))
@@ -76,12 +76,12 @@ def tile_picked_jkeyeglesdkdif_none_p_kernel(
         load_w1(1)
         n1_t = load_list("n1_t", n1)
         load_w1(2)
+        two_t = load_list("two_t", two)
         load_w1(3)
         ds_rows = d_scales[0].bitcast(I32)
         for e in range(2):
             nc.sync.dma_start(ds_win[e:P:16, :].bitcast(I32), ds_rows[e:16:2, :])
         kidx_t = load_list("kidx_t", kidx)
-        two_t = load_list("two_t", two)
         dw_win = tile("dw_win", [P, G], U32)
         nc.sync.dma_start(dw_win[:].bitcast(I32), d_words[0].rearrange("p n r -> p (n r)").bitcast(I32))
         tau2_c = load_col("tau2_c", tau2)
@@ -94,11 +94,13 @@ def tile_picked_jkeyeglesdkdif_none_p_kernel(
         n4_t = load_list("n4_t", n4)
         n5_t = load_list("n5_t", n5)
 
+        ds_p = tile("ds_p", [P, H], U8)
+        nc.gpsimd.memset(ds_p[:].bitcast(I32), 0)
         ident = tile("ident", [P, P], F32)
         make_identity(nc, ident[:])
         s_win = [tile(f"s_win{t}", [P, SW], F32) for t in range(R)]
         for t in range(R):
-            nc.gpsimd.memset(s_win[t][:, S:], 0.0)
+            nc.vector.memset(s_win[t][:, S:], 0.0)
 
         xs1 = tile("xs1", [P, S], U8)
         nc.vector.tensor_copy(xs1[:], xs_win[:].indirect(offs_t[:]))
@@ -152,16 +154,14 @@ def tile_picked_jkeyeglesdkdif_none_p_kernel(
         nc.vector.tensor_copy(
             ds_d[:].rearrange("p (t m) -> p m t", t=R), ds_g[:].rearrange("p (m t) -> p m t", t=R)
         )
-        ds_p = tile("ds_p", [P, H], U8)
-        nc.vector.tensor_copy(ds_p[:].bitcast(I32), ds_d[:].bitcast(I32))
-        for e in range(2):
-            nc.sync.dma_start(ds_p[2 + e : P : 32, :].bitcast(I32), ds_d[16 + e : P : 32, :].bitcast(I32))
+        for r in range(4):
+            nc.sync.dma_start(ds_p[r:P:32, :].bitcast(I32), ds_d[16 * (r // 2) + r % 2 : P : 32, :].bitcast(I32))
 
         w3_raw = tile("w3_raw", [P, R, N], F32, tag="ds_d")
         nc.sync.dma_start(w3_raw[:], w3.rearrange("(p j) c -> p j c", j=R))
-        xw2 = tile("xw2", [P, S], U32, tag="top1_2")
+        xw2 = tile("xw2", [P, S], U32, tag="w1_bf2")
         nc.vector.tensor_copy(xw2[:], xw_win[:].indirect(two_t[:]))
-        xs2 = tile("xs2", [P, S], U8, tag="top1_1")
+        xs2 = tile("xs2", [P, S], U8, tag="w1_bf3")
         nc.vector.tensor_copy(xs2[:], xs_win[:].indirect(two_t[:]))
         dw_g = tile("dw_g", [P, H], U32, tag="top1_3")
         nc.vector.tensor_copy(dw_g[:], dw_win[:].indirect(kidx_t[:]))
@@ -183,7 +183,7 @@ def tile_picked_jkeyeglesdkdif_none_p_kernel(
             )
             nc.vector.tensor_scalar(nb2[:, t : t + 1], top2[t][:], tau2_c[:, t : t + 1], -1.0, MULT, MULT)
 
-        ms_ps = [bank("ms_ps0", "A3"), bank("ms_ps1", "B3")]
+        ms_ps = [bank("ms_ps0", "A3"), bank("ms_ps1", "A0")]
         for t in range(R):
             for h in range(2):
                 ea = tile(f"ea{t}{h}", [P, W // 2], F32)
@@ -224,17 +224,19 @@ def tile_picked_jkeyeglesdkdif_none_p_kernel(
         w2_c, w2_s = quantise("w2", bf[:])
         w3_c, w3_s = quantise("w3", bf3[:])
 
+        quarter = tile("quarter", [P, 1], F32)
+        nc.gpsimd.memset(quarter[:], 0.25)
         ln_t = tile("ln_t", [P, 2, 512], F32, tag="hold")
         u_t = tile("u_t", [P, 2, H], F32)
         for u in range(2):
-            nc.scalar.activation(ln_t[:, u, :], ms_ps[u][:], LN, bias=0.25)
+            nc.scalar.activation(ln_t[:, u, :], ms_ps[u][:], LN, bias=quarter[:])
             nc.vector.scalar_tensor_tensor(
                 u_t[:, :, 256 * u : 256 * (u + 1)], yt_ps[u][:].rearrange("p (h c) -> p h c", h=2), -0.5,
                 ln_t[:, u, :].rearrange("p (h c) -> p h c", h=2), MULT, ADD,
             )
         z_bf = tile("z_bf", [P, S, R], BF16, tag="top2_3")
         for h in range(2):
-            u_ps = bank(f"u_ps{h}", f"A{h}")
+            u_ps = bank(f"u_ps{h}", ["B3", "A1"][h])
             for t in range(R):
                 nc.tensor.transpose(u_ps[:, P * t : P * (t + 1)], u_t[:, h, t::R], ident[:])
             nc.vector.tensor_tensor(
@@ -243,19 +245,20 @@ def tile_picked_jkeyeglesdkdif_none_p_kernel(
             )
         z_c, z_s = quantise("z", z_bf[:])
 
-        z2f = tile("z2f", [P, R - 1, S], F32, tag="top2_3")
-        z2_bf = tile("z2_bf", [P, S, R], BF16)
+        z2_work = tile("z2_work", [P, 4 * S], F32, tag="top2_3")
+        z2f = z2_work[:, : 2 * S].rearrange("p (t c) -> p t c", t=2)
+        z2_bf = z2_work[:, 2 * S :].bitcast(BF16).rearrange("p (c t) -> p c t", t=R)
         for t in range(R):
-            ds = tile(f"ds{t}", [P, SW], F32)
+            ds = tile(f"ds{t}", [P, SW], F32, tag=["quarter", "hold", "sm0", "sm1"][t])
             nc.scalar.activation(ds[:].indirect(n3_t[:]), sm[t][:], COPY)
-            dst = z2f[:, t, :] if t < R - 1 else z2_bf[:, :, t]
+            dst = z2f[:, t, :] if t < 2 else z2_bf[:, :, t]
             nc.vector.scalar_tensor_tensor(dst, s_win[t][:, :S], gkh[:, t : t + 1], ds[:, :S], MULT, ADD)
-            if t == R - 2:
+            if t == 1:
                 nc.vector.tensor_copy(
-                    z2_bf[:, :, : R - 1].rearrange("p (c i) t -> p c t i", i=4),
-                    z2f[:].rearrange("p t (c i) -> p c t i", i=4),
+                    z2_bf[:, :, :2].rearrange("p (c i) t -> p c t i", i=4),
+                    z2f.rearrange("p t (c i) -> p c t i", i=4),
                 )
-        z2_c, z2_s = quantise("z2", z2_bf[:])
+        z2_c, z2_s = quantise("z2", z2_bf)
 
         h_ps = [bank(f"h_ps{m}", tag) for m, tag in enumerate(["A2", "B0", "A3", "B1"])]
         for m in range(R):

@@ -66,7 +66,7 @@ def tile_picked_jkeyeglesdkdif_none_p_kernel(
         offs_t = load_list("offs_t", offs)
         xs_rows = x_scales[0].bitcast(I32)
         for q in range(4):
-            (nc.sync if q == 0 else nc.scalar).dma_start(xs_win[32 * q : 32 * q + 4, :].bitcast(I32), xs_rows[4 * q : 4 * q + 4, :])
+            (nc.sync if q < 2 else nc.scalar).dma_start(xs_win[32 * q : 32 * q + 4, :].bitcast(I32), xs_rows[4 * q : 4 * q + 4, :])
         load_w1(0)
         xw_win = tile("xw_win", [P, T], U32)
         nc.sync.dma_start(xw_win[:].bitcast(I32), x_words[0].rearrange("p n r -> p (n r)").bitcast(I32))
@@ -100,7 +100,7 @@ def tile_picked_jkeyeglesdkdif_none_p_kernel(
         make_identity(nc, ident[:])
         s_win = [tile(f"s_win{t}", [P, SW], F32) for t in range(R)]
         for t in range(R):
-            nc.vector.memset(s_win[t][:, S:], 0.0)
+            nc.gpsimd.memset(s_win[t][:, S:], 0.0)
 
         xs1 = tile("xs1", [P, S], U8)
         nc.vector.tensor_copy(xs1[:], xs_win[:].indirect(offs_t[:]))
@@ -133,7 +133,10 @@ def tile_picked_jkeyeglesdkdif_none_p_kernel(
 
         for t in range(2):
             bf, dst, src = interleave(w1_raw[t], f"w1_bf{t}")
-            nc.scalar.activation(dst, src, COPY)
+            if t == 0:
+                nc.vector.tensor_copy(dst, src)
+            else:
+                nc.scalar.activation(dst, src, COPY)
             codes, scales = quantise(f"w1_{t}", bf[:])
             if t == 0:
                 nc.vector.tensor_copy(xw1[:], xw_win[:].indirect(offs_t[:]))
@@ -245,6 +248,7 @@ def tile_picked_jkeyeglesdkdif_none_p_kernel(
             )
         z_c, z_s = quantise("z", z_bf[:])
 
+        halves = [slice(0, P), slice(P, S)]
         z2_work = tile("z2_work", [P, 4 * S], F32, tag="top2_3")
         z2f = z2_work[:, : 2 * S].rearrange("p (t c) -> p t c", t=2)
         z2_bf = z2_work[:, 2 * S :].bitcast(BF16).rearrange("p (c t) -> p c t", t=R)
@@ -252,13 +256,16 @@ def tile_picked_jkeyeglesdkdif_none_p_kernel(
             ds = tile(f"ds{t}", [P, SW], F32, tag=["quarter", "hold", "sm0", "sm1"][t])
             nc.scalar.activation(ds[:].indirect(n3_t[:]), sm[t][:], COPY)
             dst = z2f[:, t, :] if t < 2 else z2_bf[:, :, t]
-            nc.vector.scalar_tensor_tensor(dst, s_win[t][:, :S], gkh[:, t : t + 1], ds[:, :S], MULT, ADD)
+            for cols in [slice(0, S)] if t < R - 1 else halves:
+                nc.vector.scalar_tensor_tensor(
+                    dst[:, cols], s_win[t][:, cols], gkh[:, t : t + 1], ds[:, cols], MULT, ADD
+                )
             if t == 1:
                 nc.vector.tensor_copy(
                     z2_bf[:, :, :2].rearrange("p (c i) t -> p c t i", i=4),
                     z2f.rearrange("p t (c i) -> p c t i", i=4),
                 )
-        z2_c, z2_s = quantise("z2", z2_bf)
+        z2_q = [quantise(f"z2_{h}", z2_bf[:, cols, :]) for h, cols in enumerate(halves)]
 
         h_ps = [bank(f"h_ps{m}", tag) for m, tag in enumerate(["A2", "B0", "A3", "B1"])]
         for m in range(R):
@@ -270,10 +277,11 @@ def tile_picked_jkeyeglesdkdif_none_p_kernel(
         h_win = []
         for m in range(R):
             cols = slice(P * m, P * (m + 1))
-            nc.tensor.matmul_mx(
-                out=h_ps[m][:, :S], lhsT=w3_c[:, cols].bitcast(FP8X4), lhsT_scale=w3_s[:, cols],
-                rhs=z2_c[:].bitcast(FP8X4), rhs_scale=z2_s[:], start=False, stop=True,
-            )
+            for h, (z2_c, z2_s) in enumerate(z2_q):
+                nc.tensor.matmul_mx(
+                    out=h_ps[m][:, halves[h]], lhsT=w3_c[:, cols].bitcast(FP8X4), lhsT_scale=w3_s[:, cols],
+                    rhs=z2_c[:].bitcast(FP8X4), rhs_scale=z2_s[:], start=False, stop=(h == 1),
+                )
             h_win.append(tile(f"h_win{m}", [P, S], F32))
             nc.vector.tensor_copy(h_win[m][:], h_ps[m][:, :S])
 

@@ -133,10 +133,7 @@ def tile_picked_jkeyeglesdkdif_none_p_kernel(
 
         for t in range(2):
             bf, dst, src = interleave(w1_raw[t], f"w1_bf{t}")
-            if t == 0:
-                nc.vector.tensor_copy(dst, src)
-            else:
-                nc.scalar.activation(dst, src, COPY)
+            nc.scalar.activation(dst, src, COPY)
             codes, scales = quantise(f"w1_{t}", bf[:])
             if t == 0:
                 nc.vector.tensor_copy(xw1[:], xw_win[:].indirect(offs_t[:]))

from contextlib import ExitStack

import concourse.mybir as mybir
from concourse.masks import make_identity

K, T, S, N, H, G, W, U = 512, 1024, 256, 512, 512, 2048, 1024, 192
FLOPS = 2 * (K * H * S + K * H * S + H * N * S + H * N * S)

F32 = mybir.dt.float32
BF16 = mybir.dt.bfloat16
I32 = mybir.dt.int32
U32 = mybir.dt.uint32
U16 = mybir.dt.uint16
U8 = mybir.dt.uint8
FP8X4 = mybir.dt.float8_e4m3fn_x4
MULT = mybir.AluOpType.mult
ADD = mybir.AluOpType.add
MAX = mybir.AluOpType.max
COPY = mybir.ActivationFunctionType.Copy
EXP = mybir.ActivationFunctionType.Exp
LN = mybir.ActivationFunctionType.Ln

P = 128
R = 4
YW = 1024
SW = 512


def tile_picked_jkeyeglesdkdif_none_p_kernel(
    tc, x_words, x_scales, w1, d_words, d_scales, tau, tau2, gn, gk, w2, w3, offs, kidx, two, n1, n2, n3, n4, n5, out
):
    nc = tc.nc
    with ExitStack() as ctx:
        lists = ctx.enter_context(tc.tile_pool(name="lists", bufs=1))
        sb = ctx.enter_context(tc.tile_pool(name="sb", bufs=1))
        ps = ctx.enter_context(tc.psum_pool(name="ps", bufs=1))

        def tile(name, shape, dtype, tag=None):
            return sb.tile(shape, dtype, name=name, tag=tag or name, align_bytes=64)

        def bank(name, tag):
            return ps.tile([P, 512], F32, name=name, tag=tag)

        def load_list(name, src):
            t = lists.tile(list(src.shape), U16, name=name, tag=name)
            nc.sync.dma_start(t[:], src)
            return t

        def load_col(name, src):
            t = tile(name, [P, R], F32)
            nc.sync.dma_start(t[:], src.rearrange("(p t) o -> p (t o)", t=R))
            return t

        xs_win = tile("xs_win", [P, T], U8)
        nc.gpsimd.memset(xs_win[:].bitcast(I32), 0)
        ds_win = tile("ds_win", [P, G], U8)
        nc.vector.memset(ds_win[:].bitcast(I32), 0)
        y_win = [tile(f"y_win{t}", [P, YW], F32) for t in range(R)]
        for t in range(R):
            nc.vector.memset(y_win[t][:, 3 * S :], 0.0)
        w1_raw = [y_win[t][:, S : 3 * S].rearrange("p (j c) -> p j c", j=R) for t in range(R)]

        def load_w1(t):
            nc.sync.dma_start(w1_raw[t], w1.rearrange("(p j) c -> p j c", j=R)[:, :, P * t : P * (t + 1)])

        offs_t = load_list("offs_t", offs)
        xs_rows = x_scales[0].bitcast(I32)
        for q in range(4):
            (nc.sync if q < 2 else nc.scalar).dma_start(xs_win[32 * q : 32 * q + 4, :].bitcast(I32), xs_rows[4 * q : 4 * q + 4, :])
        load_w1(0)
        xw_win = tile("xw_win", [P, T], U32)
        nc.sync.dma_start(xw_win[:].bitcast(I32), x_words[0].rearrange("p n r -> p (n r)").bitcast(I32))
        tau_c = tile("tau_c", [P, R], F32)
        with nc.allow_non_contiguous_dma(reason="one value a row, rows in plain order"):
            nc.sync.dma_start(tau_c[:], tau.rearrange("(t p) o -> p (t o)", p=P))
        load_w1(1)
        n1_t = load_list("n1_t", n1)
        load_w1(2)
        two_t = load_list("two_t", two)
        load_w1(3)
        ds_rows = d_scales[0].bitcast(I32)
        for e in range(2):
            nc.sync.dma_start(ds_win[e:P:16, :].bitcast(I32), ds_rows[e:16:2, :])
        kidx_t = load_list("kidx_t", kidx)
        dw_win = tile("dw_win", [P, G], U32)
        nc.sync.dma_start(dw_win[:].bitcast(I32), d_words[0].rearrange("p n r -> p (n r)").bitcast(I32))
        tau2_c = load_col("tau2_c", tau2)
        n2_t = load_list("n2_t", n2)
        gk_c = load_col("gk_c", gk)
        gn_c = load_col("gn_c", gn)
        w2_raw = tile("w2_raw", [P, R, N], F32)
        nc.sync.dma_start(w2_raw[:], w2.rearrange("(p j) c -> p j c", j=R))
        n3_t = load_list("n3_t", n3)
        n4_t = load_list("n4_t", n4)
        n5_t = load_list("n5_t", n5)

        ds_p = tile("ds_p", [P, H], U8)
        nc.gpsimd.memset(ds_p[:].bitcast(I32), 0)
        ident = tile("ident", [P, P], F32)
        make_identity(nc, ident[:])
        s_win = [tile(f"s_win{t}", [P, SW], F32) for t in range(R)]
        for t in range(R):
            nc.gpsimd.memset(s_win[t][:, S:], 0.0)

        xs1 = tile("xs1", [P, S], U8)
        nc.vector.tensor_copy(xs1[:], xs_win[:].indirect(offs_t[:]))

        def interleave(raw, name, tag=None):
            bf = tile(name, [P, raw.shape[2], R], BF16, tag=tag)
            return bf, bf[:].rearrange("p (c i) j -> p c j i", i=4), raw.rearrange("p j (c i) -> p c j i", i=4)

        def quantise(name, bf):
            width = bf.shape[1]
            codes = tile(name + "_c", [P, width], U32)
            scales = tile(name + "_s", [P, width], U8)
            nc.vector.quantize_mx(out=codes[:].bitcast(FP8X4), scales=scales[:], in_=bf.rearrange("p c j -> p (c j)"))
            return codes, scales

        top1 = [tile(f"top1_{t}", [P, 1], F32) for t in range(R)]
        nb1 = tile("nb1", [P, R], F32)
        xw1 = tile("xw1", [P, S], U32)

        def project(t, w1_c, w1_s):
            y_ps = bank(f"y_ps{t}", f"A{t}")
            nc.tensor.matmul_mx(
                out=y_ps[:, :S], lhsT=w1_c.bitcast(FP8X4), lhsT_scale=w1_s,
                rhs=xw1[:].bitcast(FP8X4), rhs_scale=xs1[:], start=True, stop=True,
            )
            nc.vector.tensor_scalar(
                y_win[t][:, :S], y_ps[:, :S], 1.0, None, MULT, MAX, accum_out=top1[t][:]
            )
            nc.vector.tensor_scalar(nb1[:, t : t + 1], top1[t][:], tau_c[:, t : t + 1], -1.0, MULT, MULT)

        for t in range(2):
            bf, dst, src = interleave(w1_raw[t], f"w1_bf{t}")
            nc.scalar.activation(dst, src, COPY)
            codes, scales = quantise(f"w1_{t}", bf[:])
            if t == 0:
                nc.vector.tensor_copy(xw1[:], xw_win[:].indirect(offs_t[:]))
            project(t, codes[:], scales[:])

        w1_q = []
        for t in range(2, R):
            bf, dst, src = interleave(w1_raw[t], f"w1_bf{t}")
            nc.vector.tensor_copy(dst, src)
            w1_q.append(bf)
        for t in range(2, R):
            codes, scales = quantise(f"w1_{t}", w1_q[t - 2][:])
            project(t, codes[:], scales[:])

        ds_g = tile("ds_g", [P, H], U8, tag="top1_3")
        nc.vector.tensor_copy(ds_g[:], ds_win[:].indirect(kidx_t[:]))
        ds_d = tile("ds_d", [P, H], U8)
        nc.vector.tensor_copy(
            ds_d[:].rearrange("p (t m) -> p m t", t=R), ds_g[:].rearrange("p (m t) -> p m t", t=R)
        )
        for r in range(4):
            nc.sync.dma_start(ds_p[r:P:32, :].bitcast(I32), ds_d[16 * (r // 2) + r % 2 : P : 32, :].bitcast(I32))

        w3_raw = tile("w3_raw", [P, R, N], F32, tag="ds_d")
        nc.sync.dma_start(w3_raw[:], w3.rearrange("(p j) c -> p j c", j=R))
        xw2 = tile("xw2", [P, S], U32, tag="w1_bf2")
        nc.vector.tensor_copy(xw2[:], xw_win[:].indirect(two_t[:]))
        xs2 = tile("xs2", [P, S], U8, tag="w1_bf3")
        nc.vector.tensor_copy(xs2[:], xs_win[:].indirect(two_t[:]))
        dw_g = tile("dw_g", [P, H], U32, tag="top1_3")
        nc.vector.tensor_copy(dw_g[:], dw_win[:].indirect(kidx_t[:]))
        dw_d = tile("dw_d", [P, H], U32)
        nc.vector.tensor_copy(
            dw_d[:].rearrange("p (t m) -> p m t", t=R), dw_g[:].rearrange("p (m t) -> p m t", t=R)
        )
        top2 = [tile(f"top2_{t}", [P, 1], F32) for t in range(R)]
        nb2 = tile("nb2", [P, R], F32, tag="hold")
        for t in range(R):
            s_ps = bank(f"s_ps{t}", ["A0", "A1", "A2", "B3"][t])
            cols = slice(P * t, P * (t + 1))
            nc.tensor.matmul_mx(
                out=s_ps[:, :S], lhsT=dw_d[:, cols].bitcast(FP8X4), lhsT_scale=ds_p[:, cols],
                rhs=xw2[:].bitcast(FP8X4), rhs_scale=xs2[:], start=True, stop=True,
            )
            nc.vector.tensor_scalar(
                s_win[t][:, :S], s_ps[:, :S], 0.0625, None, MULT, MAX, accum_out=top2[t][:]
            )
            nc.vector.tensor_scalar(nb2[:, t : t + 1], top2[t][:], tau2_c[:, t : t + 1], -1.0, MULT, MULT)

        ms_ps = [bank("ms_ps0", "A3"), bank("ms_ps1", "A0")]
        for t in range(R):
            for h in range(2):
                ea = tile(f"ea{t}{h}", [P, W // 2], F32)
                nc.scalar.activation(
                    ea[:], y_win[t][:].indirect(n1_t[:, 32 * h : 32 * (h + 1)]), EXP,
                    bias=nb1[:, t : t + 1], scale=tau_c[:, t : t + 1],
                )
                blk = 2 * h + t % 2
                for e in range(4):
                    nc.tensor.matmul(
                        ms_ps[t // 2][:, P * blk : P * (blk + 1)], lhsT=ea[:, e :: 4], rhs=ident[:],
                        start=(e == 0), stop=(e == 3), is_transpose=True,
                    )

        yt_ps = [bank("yt_ps0", "B1"), bank("yt_ps1", "B2")]
        for t in range(R):
            for h in range(2):
                blk = 2 * h + t % 2
                nc.tensor.transpose(yt_ps[t // 2][:, P * blk : P * (blk + 1)], y_win[t][:, P * h : P * (h + 1)], ident[:])

        gk2 = tile("gk2", [P, R], F32)
        nc.vector.tensor_scalar(gk2[:], gk_c[:], 2.0, None, MULT)
        gkh = tile("gkh", [P, R], F32)
        nc.vector.tensor_scalar(gkh[:], gk_c[:], -0.5, None, MULT)
        sm = []
        for t in range(R):
            ea2 = tile(f"ea2{t}", [P, S], F32)
            nc.scalar.activation(
                ea2[:], s_win[t][:].indirect(n2_t[:]), EXP, bias=nb2[:, t : t + 1], scale=tau2_c[:, t : t + 1]
            )
            sm.append(tile(f"sm{t}", [P, S], F32))
            nc.vector.scalar_tensor_tensor(sm[t][:], s_win[t][:, :S], gk2[:, t : t + 1], ea2[:], MULT, MULT)

        bf, dst, src = interleave(w2_raw[:], "w2_bf", "top2_2")
        nc.vector.tensor_copy(dst, src)
        bf3, dst, src = interleave(w3_raw[:], "w3_bf", "top2_3")
        nc.vector.tensor_copy(dst, src)
        w2_c, w2_s = quantise("w2", bf[:])
        w3_c, w3_s = quantise("w3", bf3[:])

        quarter = tile("quarter", [P, 1], F32)
        nc.gpsimd.memset(quarter[:], 0.25)
        ln_t = tile("ln_t", [P, 2, 512], F32, tag="hold")
        u_t = tile("u_t", [P, 2, H], F32)
        for u in range(2):
            nc.scalar.activation(ln_t[:, u, :], ms_ps[u][:], LN, bias=quarter[:])
            nc.vector.scalar_tensor_tensor(
                u_t[:, :, 256 * u : 256 * (u + 1)], yt_ps[u][:].rearrange("p (h c) -> p h c", h=2), -0.5,
                ln_t[:, u, :].rearrange("p (h c) -> p h c", h=2), MULT, ADD,
            )
        z_bf = tile("z_bf", [P, S, R], BF16, tag="top2_3")
        for h in range(2):
            u_ps = bank(f"u_ps{h}", ["B3", "A1"][h])
            for t in range(R):
                nc.tensor.transpose(u_ps[:, P * t : P * (t + 1)], u_t[:, h, t::R], ident[:])
            nc.vector.tensor_tensor(
                z_bf[:, P * h : P * (h + 1), :], u_ps[:].rearrange("p (t j) -> p j t", t=R),
                gn_c[:].unsqueeze(1).to_broadcast([P, P, R]), MULT,
            )
        z_c, z_s = quantise("z", z_bf[:])

        halves = [slice(0, P), slice(P, S)]
        z2_work = tile("z2_work", [P, 4 * S], F32, tag="top2_3")
        z2f = z2_work[:, : 2 * S].rearrange("p (t c) -> p t c", t=2)
        z2_bf = z2_work[:, 2 * S :].bitcast(BF16).rearrange("p (c t) -> p c t", t=R)
        for t in range(R):
            ds = tile(f"ds{t}", [P, SW], F32, tag=["quarter", "hold", "sm0", "sm1"][t])
            nc.scalar.activation(ds[:].indirect(n3_t[:]), sm[t][:], COPY)
            dst = z2f[:, t, :] if t < 2 else z2_bf[:, :, t]
            for cols in [slice(0, S)] if t < R - 1 else halves:
                nc.vector.scalar_tensor_tensor(
                    dst[:, cols], s_win[t][:, cols], gkh[:, t : t + 1], ds[:, cols], MULT, ADD
                )
            if t == 1:
                nc.vector.tensor_copy(
                    z2_bf[:, :, :2].rearrange("p (c i) t -> p c t i", i=4),
                    z2f.rearrange("p t (c i) -> p c t i", i=4),
                )
        z2_q = [quantise(f"z2_{h}", z2_bf[:, cols, :]) for h, cols in enumerate(halves)]

        h_ps = [bank(f"h_ps{m}", tag) for m, tag in enumerate(["A2", "B0", "A3", "B1"])]
        for m in range(R):
            cols = slice(P * m, P * (m + 1))
            nc.tensor.matmul_mx(
                out=h_ps[m][:, :S], lhsT=w2_c[:, cols].bitcast(FP8X4), lhsT_scale=w2_s[:, cols],
                rhs=z_c[:].bitcast(FP8X4), rhs_scale=z_s[:], start=True, stop=False,
            )
        h_win = []
        for m in range(R):
            cols = slice(P * m, P * (m + 1))
            for h, (z2_c, z2_s) in enumerate(z2_q):
                nc.tensor.matmul_mx(
                    out=h_ps[m][:, halves[h]], lhsT=w3_c[:, cols].bitcast(FP8X4), lhsT_scale=w3_s[:, cols],
                    rhs=z2_c[:].bitcast(FP8X4), rhs_scale=z2_s[:], start=False, stop=(h == 1),
                )
            h_win.append(tile(f"h_win{m}", [P, S], F32))
            nc.vector.tensor_copy(h_win[m][:], h_ps[m][:, :S])

        ra = []

        def fetch(m):
            old = tile(f"old{m}", [P, U], F32)
            nc.scalar.activation(old[:], h_win[m][:].indirect(n4_t[:]), COPY)
            pa = tile(f"pa{m}", [P, U], F32)
            nc.scalar.activation(pa[:], h_win[m][:].indirect(n5_t[:]), COPY)
            ra.append(tile(f"ra{m}", [P, U], F32))
            nc.vector.scalar_tensor_tensor(ra[m][:], pa[:], -0.5, old[:], MULT, ADD)

        def put(m):
            nc.scalar.activation(h_win[m][:].indirect(n4_t[:]), ra[m][:], COPY)
            nc.sync.dma_start(out[P * m : P * (m + 1), :], h_win[m][:])

        fetch(0)
        for m in range(1, R):
            fetch(m)
            put(m - 1)
        put(R - 1)
